import numpy as np
import ml_dtypes


def mxq(x, axis, fmt="e4m3"):
    dtype, down = {"e4m3": (ml_dtypes.float8_e4m3fn, 7), "e5m2": (ml_dtypes.float8_e5m2, 14)}[fmt]
    v = np.moveaxis(np.asarray(x, np.float32).astype(ml_dtypes.bfloat16).astype(np.float64), axis, -1)
    blocks = v.reshape(v.shape[:-1] + (-1, 32))
    amax = np.abs(blocks).max(-1, keepdims=True)
    byte = np.maximum(np.where(amax > 0, np.frexp(amax)[1] - 1 + 127, 0) - down, 1)
    scale = np.exp2(byte - 127.0)
    codes = (blocks / scale).astype(np.float32).astype(dtype).astype(np.float64)
    return np.moveaxis((codes * scale).reshape(v.shape), -1, axis)


WIDE = False


def mx_kscale(k):
    if not WIDE:
        return np.ones(k)
    levels = np.array([10, -10, 5, -5, 0])
    if k % 512:
        return np.exp2(np.random.permutation(np.resize(levels, k // 32))).repeat(32)
    a = np.empty((k // 512, 16))
    for p in range(k // 512):
        a[p, :8] = np.random.permutation(np.resize(levels, 8))
        for g in range(8):
            far = levels[np.abs(levels - a[p, g]) >= 10]
            a[p, g + 8] = far[np.random.randint(len(far))]
    return np.exp2(a.ravel()).repeat(32)


def f64(x):
    return np.asarray(x).astype(np.float64)


def striped(idx):
    return np.tile(idx.reshape(-1, 16).T, (8, 1)).astype(np.uint16)


def unstriped(offs):
    return offs[:16].T.reshape(-1).astype(np.int64)


E2M1 = np.array([0.0, 0.5, 1.0, 1.5, 2.0, 3.0, 4.0, 6.0, -0.0, -0.5, -1.0, -1.5, -2.0, -3.0, -4.0, -6.0])


def pack_weight(w, fmt):
    k, n = w.shape
    w = f64(np.asarray(w, np.float32).astype(ml_dtypes.bfloat16)).reshape(k // 32, 32, n)
    amax = np.abs(w).max(1)
    if fmt == "e4m3":
        byte = np.frexp(amax)[1] - 1 + 127 - 7
    else:
        mant, ex = np.frexp(amax / 6.0)
        byte = np.where(mant > 0.5, ex, ex - 1) + 127
    byte = np.clip(np.where(amax > 0, byte, 1), 1, 254)
    scaled = (w * np.exp2(127.0 - byte)[:, None, :]).reshape(k, n).astype(np.float32)
    by_word = np.ascontiguousarray(scaled.reshape(k // 512, 128, 4, n).transpose(0, 1, 3, 2))
    if fmt == "e4m3":
        words = by_word.astype(ml_dtypes.float8_e4m3fn).view(np.uint8)
    else:
        c = by_word.astype(ml_dtypes.float4_e2m1fn).view(np.uint8) & 0xF
        words = (c[..., 0::2] | (c[..., 1::2] << 4)).reshape(k // 512, 128, 2 * n)
    return np.ascontiguousarray(words), np.ascontiguousarray(byte.astype(np.uint8).reshape(k // 512, 16, n))


def unpack_weight(words, scales, fmt):
    g, _, n = scales.shape
    words = np.ascontiguousarray(words).reshape(g, 128, n, -1)
    if fmt == "e4m3":
        vals = words.view(ml_dtypes.float8_e4m3fn).astype(np.float64)
    else:
        nib = np.empty((g, 128, n, 4), np.uint8)
        nib[..., 0::2] = words & 0xF
        nib[..., 1::2] = words >> 4
        vals = E2M1[nib]
    vals = vals * np.repeat(np.exp2(scales.astype(np.float64) - 127.0), 8, axis=1)[..., None]
    return vals.transpose(0, 1, 3, 2).reshape(g * 512, n)


def gelu(v):
    return 0.5 * v * (1.0 + np.tanh(np.sqrt(2.0 / np.pi) * (v + 0.044715 * v**3)))


def twice(P):
    return np.random.permutation(np.repeat(np.arange(P), 2))


def bf(x):
    return np.asarray(x, np.float32).astype(ml_dtypes.bfloat16)


def planes(Y):
    n, m = Y.shape
    b = f64(bf(Y)).reshape(n // 32, 32, m)
    amax = np.abs(b).max(1)
    byte = np.clip(np.where(amax > 0, np.frexp(amax)[1] - 1 + 127 - 7, 1), 1, 254)
    codes = (b * np.exp2(127.0 - byte)[:, None, :]).reshape(n, m).astype(np.float32).astype(ml_dtypes.float8_e4m3fn).view(np.uint8)
    words = codes.reshape(n // 512, 128, 4, m).transpose(0, 1, 3, 2)
    return np.ascontiguousarray(words), np.ascontiguousarray(byte.astype(np.uint8).reshape(n // 512, 16, m))


K, T, S, P, H = 1536, 2048, 1024, 512, 1024


def setup_inputs():
    n = np.random.standard_normal
    s = mx_kscale(K)[:, None]
    u = mx_kscale(H)[:, None]
    d = {}
    d["tab_words"], d["tab_scales"] = pack_weight(n((K, T)) * s, "e4m3")
    d["offs"] = striped(np.random.permutation(T)[:S])
    d["w1"] = (n((K, H)) / K ** 0.5 / s * u.T).astype(np.float32)
    d["b1"] = (0.5 * n(H) * u[:, 0]).astype(np.float32)
    d["pos1"] = striped(np.random.permutation(S)[:P])
    d["pos2"] = striped(np.random.permutation(S)[:P])
    d["w2_words"], d["w2_scales"] = pack_weight(n((H, H)) / H ** 0.5 / u, "e2m1")
    d["w3"] = (n((H, H)) / H ** 0.5 / u).astype(np.float32)
    d["pos3"] = striped(twice(P))
    d["hg"] = (1.2 * np.exp(0.3 * n(H)) / u[:, 0]).astype(np.float32)
    d["gain"] = np.exp(0.8 * n(H)).astype(np.float32)
    return d


def reference(tab_words, tab_scales, offs, w1, b1, pos1, pos2, w2_words, w2_scales, w3, pos3, hg, gain):
    v = unpack_weight(tab_words, tab_scales, "e4m3")[:, unstriped(offs)]
    h = (mxq(f64(w1), 0, "e4m3").T @ v) + f64(b1)[:, None]
    x1 = mxq(h[:, unstriped(pos1)], 0, "e4m3")
    x2 = mxq(h[:, unstriped(pos2)], 0, "e4m3")
    first = unpack_weight(w2_words, w2_scales, "e2m1").T @ x1
    second = mxq(f64(w3), 0, "e4m3").T @ x2
    pad = np.minimum(first, second)
    q = f64(hg)[:, None] * h
    own = 0.5 * q * (1.0 + np.tanh((2.0 / np.pi) ** 0.5 * (q + 0.044715 * q ** 3)))
    y = f64(gain)[:, None] * (own + pad[:, unstriped(pos3)])
    words, scales = planes(y)
    return y, words, scales

@@ -1,0 +1,387 @@
+from contextlib import ExitStack
+
+import concourse.mybir as mybir
+
+K, T, S, PADS, H = 1536, 2048, 1024, 512, 1024
+FLOPS = 2 * K * H * S + 2 * 2 * H * H * PADS
+
+F32 = mybir.dt.float32
+BF16 = mybir.dt.bfloat16
+I32 = mybir.dt.int32
+U32 = mybir.dt.uint32
+U16 = mybir.dt.uint16
+U8 = mybir.dt.uint8
+E4M3 = mybir.dt.float8_e4m3fn_x4
+E2M1 = mybir.dt.float4_e2m1fn_x4
+ACT = mybir.ActivationFunctionType
+ALU = mybir.AluOpType
+
+P = 128
+PACK = 4
+GROUP = P * PACK
+BANK = 512
+K_PASSES = K // GROUP
+H_GROUPS = H // GROUP
+HALVES = S // BANK
+CHUNKS = [[(0, 512), (512, 512)], [(0, 512), (512, 256), (768, 256)]]
+PAD_WINDOW = PADS + 32
+LIST_ROWS = 16
+
+
+def tile_list_bonsai_vigour_features_kernel(
+    tc, tab_words, tab_scales, offs, w1, b1, pos1, pos2, w2_words, w2_scales, w3, pos3, hg, gain, out_0, out_1, out_2
+):
+    nc = tc.nc
+    with ExitStack() as ctx:
+        keep = ctx.enter_context(tc.tile_pool(name="keep", bufs=1))
+        ring = ctx.enter_context(tc.tile_pool(name="ring", bufs=1))
+        psum = ctx.enter_context(tc.psum_pool(name="psum", bufs=8))
+
+        def copy_on(engine, out, in_):
+            if engine == "vector":
+                nc.vector.tensor_copy(out=out, in_=in_)
+            else:
+                nc.scalar.copy(out=out, in_=in_)
+
+        offs_t = keep.tile([P, S // LIST_ROWS], U16, name="offs_t")
+        pos1_t = keep.tile([P, PADS // LIST_ROWS], U16, name="pos1_t")
+        pos2_t = keep.tile([P, PADS // LIST_ROWS], U16, name="pos2_t")
+        pos3_t = keep.tile([P, S // LIST_ROWS], U16, name="pos3_t")
+        tab_w = [keep.tile([P, T], I32, name=f"tab_w{a}", align_bytes=64) for a in range(K_PASSES)]
+        tab_s = keep.tile([P, T], U8, name="tab_s", align_bytes=64)
+        got_w = [keep.tile([P, S], U32, name=f"got_w{a}", align_bytes=64) for a in range(K_PASSES)]
+        got_s = keep.tile([P, S], U8, name="got_s", align_bytes=64)
+        w2_raw = keep.tile([P, H_GROUPS, 2 * H], U8, name="w2_raw", align_bytes=64)
+        w2_raw_s = keep.tile([P, H_GROUPS, H], U8, name="w2_raw_s", align_bytes=64)
+        w2_c = keep.tile([P, H_GROUPS, 2 * H], U8, name="w2_c", align_bytes=64)
+        w2_s = keep.tile([P, H_GROUPS, H], U8, name="w2_s", align_bytes=64)
+        b1_t = keep.tile([P, H_GROUPS, PACK], F32, name="b1_t")
+        hg_t = keep.tile([P, H_GROUPS, PACK], F32, name="hg_t")
+        gain_t = keep.tile([P, H_GROUPS, PACK], F32, name="gain_t")
+        h = [[keep.tile([P, S], F32, name=f"h{g}{t}") for t in range(PACK)] for g in range(H_GROUPS)]
+        y = [[keep.tile([P, PACK, n], F32, name=f"y{g}{j0}") for j0, n in CHUNKS[g]] for g in range(H_GROUPS)]
+        pad = [[keep.tile([P, PAD_WINDOW], F32, name=f"pad{g}{t}") for t in range(PACK)] for g in range(H_GROUPS)]
+        x_c = [[keep.tile([P, PADS], U32, name=f"x_c{i}{g}", align_bytes=64) for g in range(H_GROUPS)] for i in range(2)]
+        x_s = [[keep.tile([P, PADS], U8, name=f"x_s{i}{g}", align_bytes=64) for g in range(H_GROUPS)] for i in range(2)]
+        y_s = [keep.tile([P, S], U8, name=f"y_s{g}", align_bytes=64) for g in range(H_GROUPS)]
+        warm = keep.tile([P, 8], F32, name="warm")
+
+        nc.vector.memset(tab_s[:].bitcast(I32), 0)
+        nc.vector.memset(w2_raw_s[:].rearrange("p a c -> p (a c)").bitcast(I32), 0)
+        nc.gpsimd.memset(warm[:], 0.0)
+        nc.scalar.activation(out=warm[:, 4:5], in_=warm[:, 0:1], func=ACT.Gelu_apprx_tanh)
+        for g in range(H_GROUPS):
+            for t in range(PACK):
+                nc.gpsimd.memset(pad[g][t][:, PADS:], 0.0)
+
+        def load_weight(w, a, g, tag="raw", bufs=3):
+            raw = ring.tile([P, PACK, GROUP], F32, name="raw", tag=tag, bufs=bufs, align_bytes=64)
+            nc.sync.dma_start(
+                out=raw[:],
+                in_=w[a * GROUP : (a + 1) * GROUP, g * GROUP : (g + 1) * GROUP].rearrange("(p i) c -> p i c", i=PACK),
+            )
+            return raw
+
+        def load_table(a):
+            nc.sync.dma_start(out=tab_w[a][:], in_=tab_words[a].rearrange("p c i -> p (c i)").bitcast(I32))
+
+        def round_weight(raw, engine):
+            woven = ring.tile([P, GROUP * PACK], BF16, name="woven", tag="woven", bufs=3, align_bytes=64)
+            copy_on(
+                engine,
+                woven[:].rearrange("p (t m i) -> p m i t", t=PACK, i=PACK),
+                raw[:].rearrange("p i (m t) -> p m i t", t=PACK),
+            )
+            return woven
+
+        def round_planes(planes, engine):
+            woven = ring.tile([P, planes.shape[2] * PACK], BF16, name="woven", tag="woven", bufs=3, align_bytes=64)
+            copy_on(
+                engine,
+                woven[:].rearrange("p (c e t) -> p c t e", t=PACK, e=4),
+                planes.rearrange("p t (c e) -> p c t e", e=4),
+            )
+            return woven
+
+        def quantize_weight(woven):
+            codes = ring.tile([P, GROUP], U32, name="w_c", tag="w_c", bufs=7, align_bytes=64)
+            scales = ring.tile([P, GROUP], U8, name="w_s", tag="w_s", bufs=7, align_bytes=64)
+            nc.vector.quantize_mx(out=codes[:].bitcast(E4M3), scales=scales[:], in_=woven[:])
+            return codes, scales
+
+        def gather_table(a, j0, n):
+            nc.vector.tensor_copy(
+                out=got_w[a][:, j0 : j0 + n],
+                in_=tab_w[a][:].bitcast(U32).indirect(offs_t[:, j0 // LIST_ROWS : (j0 + n) // LIST_ROWS]),
+            )
+
+        def first_stage_pass(banks, a, codes, scales):
+            for u in range(HALVES):
+                for t in range(PACK):
+                    cols = slice(t * P, (t + 1) * P)
+                    ent = slice(u * BANK, (u + 1) * BANK)
+                    nc.tensor.matmul_mx(
+                        out=banks[t][u][:],
+                        lhsT=codes[:, cols].bitcast(E4M3),
+                        lhsT_scale=scales[:, cols],
+                        rhs=got_w[a][:, ent].bitcast(E4M3),
+                        rhs_scale=got_s[4 * a : P, ent],
+                        start=(a == 0),
+                        stop=(a == K_PASSES - 1),
+                    )
+
+        def first_stage_slice(banks, t, quantized):
+            cols = slice(t * P, (t + 1) * P)
+            for u in range(HALVES):
+                ent = slice(u * BANK, (u + 1) * BANK)
+                for a, (codes, scales) in enumerate(quantized):
+                    nc.tensor.matmul_mx(
+                        out=banks[t][u][:],
+                        lhsT=codes[:, cols].bitcast(E4M3),
+                        lhsT_scale=scales[:, cols],
+                        rhs=got_w[a][:, ent].bitcast(E4M3),
+                        rhs_scale=got_s[4 * a : P, ent],
+                        start=(a == 0),
+                        stop=(a == K_PASSES - 1),
+                    )
+
+        def new_banks():
+            return [[psum.tile([P, BANK], F32, name="bank", tag="bank") for u in range(HALVES)] for t in range(PACK)]
+
+        def add_bias(banks, g, t, u):
+            nc.scalar.activation(
+                out=h[g][t][:, u * BANK : (u + 1) * BANK], in_=banks[t][u][:], func=ACT.Identity,
+                bias=b1_t[:, g, t : t + 1],
+            )
+
+        def gelu(g, u, t):
+            j0, n = CHUNKS[g][u]
+            nc.scalar.activation(
+                out=y[g][u][:, t, :], in_=h[g][t][:, j0 : j0 + n], func=ACT.Gelu_apprx_tanh,
+                scale=hg_t[:, g, t : t + 1],
+            )
+
+        def pick(planes, g, t, places):
+            nc.vector.tensor_copy(out=planes[:, t, :], in_=h[g][t][:].indirect(places[:]))
+
+        def new_planes():
+            return ring.tile([P, PACK, BANK], BF16, name="planes", tag="planes", bufs=4, align_bytes=64)
+
+        def quantize_x(i, g, woven):
+            nc.vector.quantize_mx(out=x_c[i][g][:].bitcast(E4M3), scales=x_s[i][g][:], in_=woven[:])
+
+        def second_stage(g, t):
+            first = psum.tile([P, BANK], F32, name="bank", tag="bank")
+            second = psum.tile([P, BANK], F32, name="bank", tag="bank")
+            c0 = g * GROUP + t * P
+            for a in range(H_GROUPS):
+                nc.tensor.matmul_mx(
+                    out=first[:],
+                    lhsT=w2_c[:, a, 2 * c0 : 2 * (c0 + P)].bitcast(E2M1),
+                    lhsT_scale=w2_s[:, a, c0 : c0 + P],
+                    rhs=x_c[0][a][:].bitcast(E4M3),
+                    rhs_scale=x_s[0][a][:],
+                    start=(a == 0),
+                    stop=(a == H_GROUPS - 1),
+                )
+            for a in range(H_GROUPS):
+                codes, scales = w3q[a, g]
+                nc.tensor.matmul_mx(
+                    out=second[:],
+                    lhsT=codes[:, t * P : (t + 1) * P].bitcast(E4M3),
+                    lhsT_scale=scales[:, t * P : (t + 1) * P],
+                    rhs=x_c[1][a][:].bitcast(E4M3),
+                    rhs_scale=x_s[1][a][:],
+                    start=(a == 0),
+                    stop=(a == H_GROUPS - 1),
+                )
+            return first, second
+
+        def take_min(g, t, first, second):
+            first_sb = ring.tile([P, PADS], F32, name="first_sb", tag="first_sb", bufs=2)
+            nc.scalar.copy(out=first_sb[:], in_=first[:])
+            nc.vector.tensor_tensor(out=pad[g][t][:, :PADS], in0=second[:], in1=first_sb[:], op=ALU.min)
+
+        def finish(g, u, t, engine="scalar"):
+            j0, n = CHUNKS[g][u]
+            total = ring.tile([P, n], F32, name="total", tag="total", bufs=4)
+            nc.vector.tensor_tensor(
+                out=total[:], in0=pad[g][t][:].indirect(pos3_t[:, j0 // LIST_ROWS : (j0 + n) // LIST_ROWS]),
+                in1=y[g][u][:, t, :], op=ALU.add,
+            )
+            return total
+
+        def apply_gain(g, u, t, total, engine="scalar"):
+            if engine == "scalar":
+                nc.scalar.activation(out=y[g][u][:, t, :], in_=total[:], func=ACT.Copy, scale=gain_t[:, g, t : t + 1])
+            else:
+                nc.vector.tensor_scalar(
+                    out=y[g][u][:, t, :], in0=total[:], scalar1=gain_t[:, g, t : t + 1], scalar2=None, op0=ALU.mult
+                )
+
+        def store_y(g, u):
+            j0, n = CHUNKS[g][u]
+            nc.sync.dma_start(
+                out=out_0[g * GROUP : (g + 1) * GROUP, j0 : j0 + n].rearrange("(p t) j -> p t j", t=PACK), in_=y[g][u][:]
+            )
+
+        def quantize_y(g, u, woven):
+            j0, n = CHUNKS[g][u]
+            y_c = ring.tile([P, n], U32, name="y_c", tag="y_c", bufs=2, align_bytes=64)
+            nc.vector.quantize_mx(out=y_c[:].bitcast(E4M3), scales=y_s[g][:, j0 : j0 + n], in_=woven[:])
+            nc.sync.dma_start(
+                out=out_1[g][:, j0 : j0 + n, :].rearrange("p m t -> p (m t)").bitcast(I32), in_=y_c[:].bitcast(I32)
+            )
+
+        def store_scales(g):
+            for q in range(4):
+                (nc.scalar if g == H_GROUPS - 1 and q % 2 else nc.sync).dma_start(
+                    out=out_2[g, 4 * q : 4 * q + 4, :].bitcast(I32), in_=y_s[g][32 * q : 32 * q + 4, :].bitcast(I32)
+                )
+
+        def load_vector(vec, tile):
+            nc.sync.dma_start(out=tile[:], in_=vec.rearrange("(g p t) -> p g t", p=P, t=PACK))
+
+        raw1 = {}
+        raw3 = {}
+        nc.sync.dma_start(offs_t[:], offs)
+        load_table(0)
+        for q in range(4):
+            nc.sync.dma_start(
+                out=tab_s[32 * q : 32 * q + 4 * K_PASSES, :].bitcast(I32),
+                in_=tab_scales[:, 4 * q : 4 * q + 4, :].bitcast(I32),
+            )
+        raw1[0, 0] = load_weight(w1, 0, 0)
+        nc.sync.dma_start(out=w2_raw[:].bitcast(I32), in_=w2_words.rearrange("a p c -> p a c").bitcast(I32))
+        for q in range(4):
+            nc.sync.dma_start(
+                out=w2_raw_s[32 * q : 32 * q + 4, :, :].bitcast(I32),
+                in_=w2_scales[:, 4 * q : 4 * q + 4, :].rearrange("a r c -> r a c").bitcast(I32),
+            )
+        load_table(1)
+        raw1[1, 0] = load_weight(w1, 1, 0)
+        raw1[2, 0] = load_weight(w1, 2, 0)
+        load_table(2)
+        load_vector(b1, b1_t)
+        nc.sync.dma_start(pos1_t[:], pos1)
+        raw1[0, 1] = load_weight(w1, 0, 1, "late", 1)
+        nc.sync.dma_start(pos2_t[:], pos2)
+        raw1[1, 1] = load_weight(w1, 1, 1)
+        load_vector(hg, hg_t)
+        raw1[2, 1] = load_weight(w1, 2, 1)
+        load_vector(gain, gain_t)
+        nc.sync.dma_start(pos3_t[:], pos3)
+
+        banks = new_banks()
+        gather_table(0, 0, S)
+        woven = round_weight(raw1[0, 0], "scalar")
+        nc.vector.tensor_copy(out=got_s[:], in_=tab_s[:].indirect(offs_t[:]))
+        first_stage_pass(banks, 0, *quantize_weight(woven))
+        nc.vector.tensor_copy(
+            out=w2_c[:].bitcast(U16).rearrange("p a (g t m) -> p (a g) m t", t=PACK, m=P),
+            in_=w2_raw[:].bitcast(U16).rearrange("p a (g m t) -> p (a g) m t", t=PACK, m=P),
+        )
+        gather_table(1, 0, S)
+        woven = round_weight(raw1[1, 0], "scalar")
+        nc.vector.tensor_copy(
+            out=w2_s[:].rearrange("p a (g t m) -> p (a g) m t", t=PACK, m=P),
+            in_=w2_raw_s[:].rearrange("p a (g m t) -> p (a g) m t", t=PACK, m=P),
+        )
+        first_stage_pass(banks, 1, *quantize_weight(woven))
+        woven = round_weight(raw1[2, 0], "scalar")
+        last = quantize_weight(woven)
+        for u in range(HALVES):
+            gather_table(2, u * BANK, BANK)
+        first_stage_pass(banks, 2, *last)
+        raw3[0, 0] = load_weight(w3, 0, 0)
+        raw3[1, 0] = load_weight(w3, 1, 0, "late", 1)
+        raw3[1, 1] = load_weight(w3, 1, 1)
+
+        planes = [[new_planes() for g in range(H_GROUPS)] for i in range(2)]
+        w1q = [quantize_weight(round_weight(raw1[0, 1], "vector"))]
+
+        def pick_both(g, t):
+            pick(planes[0][g], g, t, pos1_t)
+            pick(planes[1][g], g, t, pos2_t)
+
+        def bias_both(banks, g, t):
+            for u in range(HALVES):
+                add_bias(banks, g, t, u)
+
+        for t, u in ((0, 0), (1, 0), (0, 1), (1, 1)):
+            add_bias(banks, 0, t, u)
+        pick_both(0, 0)
+        pick_both(0, 1)
+        for a in (1, 2):
+            w1q.append(quantize_weight(round_weight(raw1[a, 1], "scalar")))
+            bias_both(banks, 0, a + 1)
+            pick_both(0, a + 1)
+        banks = new_banks()
+        for t in range(PACK):
+            first_stage_slice(banks, t, w1q)
+        w3q = {}
+        w3q[0, 0] = quantize_weight(round_weight(raw3[0, 0], "scalar"))
+        for t in (0, 1):
+            bias_both(banks, 1, t)
+            pick_both(1, t)
+        for i in range(2):
+            quantize_x(i, 0, round_planes(planes[i][0][:], "scalar"))
+            bias_both(banks, 1, 2 + i)
+            pick_both(1, 2 + i)
+        w3q[1, 0] = quantize_weight(round_weight(raw3[1, 0], "scalar"))
+        raw3[0, 1] = load_weight(w3, 0, 1, "late", 1)
+        for t in range(PACK):
+            gelu(0, 0, t)
+        woven1 = round_planes(planes[0][1][:], "scalar")
+        woven2 = round_planes(planes[1][1][:], "vector")
+        quantize_x(1, 1, woven2)
+        quantize_x(0, 1, woven1)
+        woven = round_weight(raw3[0, 1], "vector")
+        totals = {}
+        woven11 = round_weight(raw3[1, 1], "scalar")
+        for t in range(PACK):
+            take_min(0, t, *second_stage(0, t))
+            if t > 0:
+                apply_gain(0, 0, t - 1, totals[t - 1])
+            totals[t] = finish(0, 0, t)
+            gelu(0, 1, t)
+        w3q[0, 1] = quantize_weight(woven)
+        w3q[1, 1] = quantize_weight(woven11)
+        apply_gain(0, 0, 3, totals[3])
+        store_y(0, 0)
+        for t in range(PACK):
+            totals[t] = finish(0, 1, t)
+            take_min(1, t, *second_stage(1, t))
+            gelu(1, 0, t)
+            if t == 0:
+                woven_y = round_planes(y[0][0][:], "scalar")
+            else:
+                apply_gain(0, 1, t - 1, totals[t - 1])
+        quantize_y(0, 0, woven_y)
+        apply_gain(0, 1, 3, totals[3])
+        store_y(0, 1)
+        for t in range(PACK):
+            totals[t] = finish(1, 0, t)
+            gelu(1, 1, t)
+            gelu(1, 2, t)
+            if t == 0:
+                woven_y = round_planes(y[0][1][:], "scalar")
+            else:
+                apply_gain(1, 0, t - 1, totals[t - 1])
+        quantize_y(0, 1, woven_y)
+        store_scales(0)
+        apply_gain(1, 0, 3, totals[3])
+        store_y(1, 0)
+        woven_y = round_planes(y[1][0][:], "scalar")
+        for t in range(PACK):
+            apply_gain(1, 1, t, finish(1, 1, t))
+        store_y(1, 1)
+        quantize_y(1, 0, woven_y)
+        woven_y = round_planes(y[1][1][:], "scalar")
+        for t in range(PACK):
+            apply_gain(1, 2, t, finish(1, 2, t))
+        store_y(1, 2)
+        quantize_y(1, 1, woven_y)
+        woven_y = round_planes(y[1][2][:], "vector")
+        quantize_y(1, 2, woven_y)
+        store_scales(1)

@@ -68,8 +68,7 @@ def tile_list_bonsai_vigour_features_kernel(
 
         nc.vector.memset(tab_s[:].bitcast(I32), 0)
         nc.vector.memset(w2_raw_s[:].rearrange("p a c -> p (a c)").bitcast(I32), 0)
-        nc.gpsimd.memset(warm[:], 0.0)
-        nc.scalar.activation(out=warm[:, 4:5], in_=warm[:, 0:1], func=ACT.Gelu_apprx_tanh)
+        nc.vector.memset(warm[:], 0.0)
         for g in range(H_GROUPS):
             for t in range(PACK):
                 nc.gpsimd.memset(pad[g][t][:, PADS:], 0.0)
@@ -104,8 +103,8 @@ def tile_list_bonsai_vigour_features_kernel(
             return woven
 
         def quantize_weight(woven):
-            codes = ring.tile([P, GROUP], U32, name="w_c", tag="w_c", bufs=7, align_bytes=64)
-            scales = ring.tile([P, GROUP], U8, name="w_s", tag="w_s", bufs=7, align_bytes=64)
+            codes = ring.tile([P, GROUP], U32, name="w_c", tag="w_c", bufs=6, align_bytes=64)
+            scales = ring.tile([P, GROUP], U8, name="w_s", tag="w_s", bufs=6, align_bytes=64)
             nc.vector.quantize_mx(out=codes[:].bitcast(E4M3), scales=scales[:], in_=woven[:])
             return codes, scales
 
@@ -227,7 +226,7 @@ def tile_list_bonsai_vigour_features_kernel(
 
         def quantize_y(g, u, woven):
             j0, n = CHUNKS[g][u]
-            y_c = ring.tile([P, n], U32, name="y_c", tag="y_c", bufs=2, align_bytes=64)
+            y_c = ring.tile([P, n], U32, name="y_c", tag="y_c", bufs=3, align_bytes=64)
             nc.vector.quantize_mx(out=y_c[:].bitcast(E4M3), scales=y_s[g][:, j0 : j0 + n], in_=woven[:])
             nc.sync.dma_start(
                 out=out_1[g][:, j0 : j0 + n, :].rearrange("p m t -> p (m t)").bitcast(I32), in_=y_c[:].bitcast(I32)
@@ -239,18 +238,23 @@ def tile_list_bonsai_vigour_features_kernel(
                     out=out_2[g, 4 * q : 4 * q + 4, :].bitcast(I32), in_=y_s[g][32 * q : 32 * q + 4, :].bitcast(I32)
                 )
 
-        def load_vector(vec, tile):
-            nc.sync.dma_start(out=tile[:], in_=vec.rearrange("(g p t) -> p g t", p=P, t=PACK))
-
         raw1 = {}
         raw3 = {}
+
+        def load_vector(queue, vec, tile):
+            queue.dma_start(out=tile[:], in_=vec.rearrange("(g p t) -> p g t", p=P, t=PACK))
+
         nc.sync.dma_start(offs_t[:], offs)
+        load_vector(nc.scalar, b1, b1_t)
         load_table(0)
         for q in range(4):
-            nc.sync.dma_start(
+            nc.scalar.dma_start(
                 out=tab_s[32 * q : 32 * q + 4 * K_PASSES, :].bitcast(I32),
                 in_=tab_scales[:, 4 * q : 4 * q + 4, :].bitcast(I32),
             )
+        nc.scalar.activation(out=warm[:, 4:5], in_=warm[:, 0:1], func=ACT.Gelu_apprx_tanh)
+        load_vector(nc.gpsimd, hg, hg_t)
+        load_vector(nc.gpsimd, gain, gain_t)
         raw1[0, 0] = load_weight(w1, 0, 0)
         nc.sync.dma_start(out=w2_raw[:].bitcast(I32), in_=w2_words.rearrange("a p c -> p a c").bitcast(I32))
         for q in range(4):
@@ -258,18 +262,15 @@ def tile_list_bonsai_vigour_features_kernel(
                 out=w2_raw_s[32 * q : 32 * q + 4, :, :].bitcast(I32),
                 in_=w2_scales[:, 4 * q : 4 * q + 4, :].rearrange("a r c -> r a c").bitcast(I32),
             )
-        load_table(1)
         raw1[1, 0] = load_weight(w1, 1, 0)
+        load_table(1)
         raw1[2, 0] = load_weight(w1, 2, 0)
         load_table(2)
-        load_vector(b1, b1_t)
-        nc.sync.dma_start(pos1_t[:], pos1)
         raw1[0, 1] = load_weight(w1, 0, 1, "late", 1)
+        nc.sync.dma_start(pos1_t[:], pos1)
         nc.sync.dma_start(pos2_t[:], pos2)
         raw1[1, 1] = load_weight(w1, 1, 1)
-        load_vector(hg, hg_t)
         raw1[2, 1] = load_weight(w1, 2, 1)
-        load_vector(gain, gain_t)
         nc.sync.dma_start(pos3_t[:], pos3)
 
         banks = new_banks()
@@ -281,21 +282,19 @@ def tile_list_bonsai_vigour_features_kernel(
             out=w2_c[:].bitcast(U16).rearrange("p a (g t m) -> p (a g) m t", t=PACK, m=P),
             in_=w2_raw[:].bitcast(U16).rearrange("p a (g m t) -> p (a g) m t", t=PACK, m=P),
         )
-        gather_table(1, 0, S)
-        woven = round_weight(raw1[1, 0], "scalar")
         nc.vector.tensor_copy(
             out=w2_s[:].rearrange("p a (g t m) -> p (a g) m t", t=PACK, m=P),
             in_=w2_raw_s[:].rearrange("p a (g m t) -> p (a g) m t", t=PACK, m=P),
         )
-        first_stage_pass(banks, 1, *quantize_weight(woven))
-        woven = round_weight(raw1[2, 0], "scalar")
-        last = quantize_weight(woven)
+        middle = quantize_weight(round_weight(raw1[1, 0], "scalar"))
+        gather_table(1, 0, S)
+        first_stage_pass(banks, 1, *middle)
+        last = quantize_weight(round_weight(raw1[2, 0], "scalar"))
         for u in range(HALVES):
             gather_table(2, u * BANK, BANK)
         first_stage_pass(banks, 2, *last)
         raw3[0, 0] = load_weight(w3, 0, 0)
         raw3[1, 0] = load_weight(w3, 1, 0, "late", 1)
-        raw3[1, 1] = load_weight(w3, 1, 1)
 
         planes = [[new_planes() for g in range(H_GROUPS)] for i in range(2)]
         w1q = [quantize_weight(round_weight(raw1[0, 1], "vector"))]
@@ -312,6 +311,9 @@ def tile_list_bonsai_vigour_features_kernel(
             add_bias(banks, 0, t, u)
         pick_both(0, 0)
         pick_both(0, 1)
+        for t in (0, 1):
+            for u in range(HALVES):
+                gelu(0, u, t)
         for a in (1, 2):
             w1q.append(quantize_weight(round_weight(raw1[a, 1], "scalar")))
             bias_both(banks, 0, a + 1)
@@ -330,40 +332,41 @@ def tile_list_bonsai_vigour_features_kernel(
             pick_both(1, 2 + i)
         w3q[1, 0] = quantize_weight(round_weight(raw3[1, 0], "scalar"))
         raw3[0, 1] = load_weight(w3, 0, 1, "late", 1)
-        for t in range(PACK):
-            gelu(0, 0, t)
         woven1 = round_planes(planes[0][1][:], "scalar")
         woven2 = round_planes(planes[1][1][:], "vector")
         quantize_x(1, 1, woven2)
         quantize_x(0, 1, woven1)
         woven = round_weight(raw3[0, 1], "vector")
+        raw3[1, 1] = load_weight(w3, 1, 1, "late", 1)
+        gelu(0, 0, 2)
+        gelu(0, 0, 3)
         totals = {}
-        woven11 = round_weight(raw3[1, 1], "scalar")
         for t in range(PACK):
             take_min(0, t, *second_stage(0, t))
-            if t > 0:
-                apply_gain(0, 0, t - 1, totals[t - 1])
             totals[t] = finish(0, 0, t)
-            gelu(0, 1, t)
-        w3q[0, 1] = quantize_weight(woven)
-        w3q[1, 1] = quantize_weight(woven11)
+            if t == 0:
+                w3q[0, 1] = quantize_weight(woven)
+            else:
+                gelu(*((0, 1, 2), (0, 1, 3), (1, 0, 0))[t - 1])
+                apply_gain(0, 0, t - 1, totals[t - 1])
+        w3q[1, 1] = quantize_weight(round_weight(raw3[1, 1], "scalar"))
         apply_gain(0, 0, 3, totals[3])
         store_y(0, 0)
         for t in range(PACK):
             totals[t] = finish(0, 1, t)
             take_min(1, t, *second_stage(1, t))
-            gelu(1, 0, t)
             if t == 0:
                 woven_y = round_planes(y[0][0][:], "scalar")
             else:
+                gelu(1, 0, t)
                 apply_gain(0, 1, t - 1, totals[t - 1])
         quantize_y(0, 0, woven_y)
         apply_gain(0, 1, 3, totals[3])
         store_y(0, 1)
         for t in range(PACK):
             totals[t] = finish(1, 0, t)
-            gelu(1, 1, t)
-            gelu(1, 2, t)
+            for u in range(1, len(CHUNKS[1])):
+                gelu(1, u, t)
             if t == 0:
                 woven_y = round_planes(y[0][1][:], "scalar")
             else:
@@ -373,15 +376,12 @@ def tile_list_bonsai_vigour_features_kernel(
         apply_gain(1, 0, 3, totals[3])
         store_y(1, 0)
         woven_y = round_planes(y[1][0][:], "scalar")
-        for t in range(PACK):
-            apply_gain(1, 1, t, finish(1, 1, t))
-        store_y(1, 1)
-        quantize_y(1, 0, woven_y)
-        woven_y = round_planes(y[1][1][:], "scalar")
-        for t in range(PACK):
-            apply_gain(1, 2, t, finish(1, 2, t))
-        store_y(1, 2)
-        quantize_y(1, 1, woven_y)
-        woven_y = round_planes(y[1][2][:], "vector")
-        quantize_y(1, 2, woven_y)
+        for u in range(1, len(CHUNKS[1])):
+            last = u == len(CHUNKS[1]) - 1
+            for t in range(PACK):
+                apply_gain(1, u, t, finish(1, u, t), "scalar")
+            store_y(1, u)
+            quantize_y(1, u - 1, woven_y)
+            woven_y = round_planes(y[1][u][:], "vector" if last else "scalar")
+        quantize_y(1, u, woven_y)
         store_scales(1)

@@ -35,7 +35,7 @@ def tile_list_bonsai_vigour_features_kernel(
     with ExitStack() as ctx:
         keep = ctx.enter_context(tc.tile_pool(name="keep", bufs=1))
         ring = ctx.enter_context(tc.tile_pool(name="ring", bufs=1))
-        psum = ctx.enter_context(tc.psum_pool(name="psum", bufs=8))
+        psum = ctx.enter_context(tc.psum_pool(name="psum", bufs=2))
 
         def copy_on(engine, out, in_):
             if engine == "vector":
@@ -88,8 +88,8 @@ def tile_list_bonsai_vigour_features_kernel(
             woven = ring.tile([P, GROUP * PACK], BF16, name="woven", tag="woven", bufs=3, align_bytes=64)
             copy_on(
                 engine,
-                woven[:].rearrange("p (t m i) -> p m i t", t=PACK, i=PACK),
-                raw[:].rearrange("p i (m t) -> p m i t", t=PACK),
+                woven[:].rearrange("p (t m i e) -> p m i t e", t=PACK, i=2, e=2),
+                raw[:].rearrange("p (i e) (m t) -> p m i t e", t=PACK, e=2),
             )
             return woven
 
@@ -145,7 +145,7 @@ def tile_list_bonsai_vigour_features_kernel(
                     )
 
         def new_banks():
-            return [[psum.tile([P, BANK], F32, name="bank", tag="bank") for u in range(HALVES)] for t in range(PACK)]
+            return [[psum.tile([P, BANK], F32, name="bank", tag=f"bank{t}") for u in range(HALVES)] for t in range(PACK)]
 
         def add_bias(banks, g, t, u):
             nc.scalar.activation(
@@ -170,8 +170,8 @@ def tile_list_bonsai_vigour_features_kernel(
             nc.vector.quantize_mx(out=x_c[i][g][:].bitcast(E4M3), scales=x_s[i][g][:], in_=woven[:])
 
         def second_stage(g, t):
-            first = psum.tile([P, BANK], F32, name="bank", tag="bank")
-            second = psum.tile([P, BANK], F32, name="bank", tag="bank")
+            first = psum.tile([P, BANK], F32, name="bank", tag="bank0")
+            second = psum.tile([P, BANK], F32, name="bank", tag="bank1")
             c0 = g * GROUP + t * P
             for a in range(H_GROUPS):
                 nc.tensor.matmul_mx(
@@ -264,7 +264,14 @@ def tile_list_bonsai_vigour_features_kernel(
             )
         raw1[1, 0] = load_weight(w1, 1, 0)
         load_table(1)
-        raw1[2, 0] = load_weight(w1, 2, 0)
+        halves = []
+        for part in range(2):
+            half = ring.tile([P, PACK, GROUP // 2], F32, name="half", tag="planes", bufs=4, align_bytes=64)
+            nc.sync.dma_start(
+                out=half[:],
+                in_=w1[2 * GROUP :, part * GROUP // 2 : (part + 1) * GROUP // 2].rearrange("(p i) c -> p i c", i=PACK),
+            )
+            halves.append(half)
         load_table(2)
         raw1[0, 1] = load_weight(w1, 0, 1, "late", 1)
         nc.sync.dma_start(pos1_t[:], pos1)
@@ -279,29 +286,36 @@ def tile_list_bonsai_vigour_features_kernel(
         nc.vector.tensor_copy(out=got_s[:], in_=tab_s[:].indirect(offs_t[:]))
         first_stage_pass(banks, 0, *quantize_weight(woven))
         nc.vector.tensor_copy(
-            out=w2_c[:].bitcast(U16).rearrange("p a (g t m) -> p (a g) m t", t=PACK, m=P),
-            in_=w2_raw[:].bitcast(U16).rearrange("p a (g m t) -> p (a g) m t", t=PACK, m=P),
+            out=w2_c[:].bitcast(U16).rearrange("p a (g t m) -> p (a g) t m", t=PACK, m=P),
+            in_=w2_raw[:].bitcast(U16).rearrange("p a (g m t) -> p (a g) t m", t=PACK, m=P),
         )
         nc.vector.tensor_copy(
-            out=w2_s[:].rearrange("p a (g t m) -> p (a g) m t", t=PACK, m=P),
-            in_=w2_raw_s[:].rearrange("p a (g m t) -> p (a g) m t", t=PACK, m=P),
+            out=w2_s[:].rearrange("p a (g t m) -> p (a g) t m", t=PACK, m=P),
+            in_=w2_raw_s[:].rearrange("p a (g m t) -> p (a g) t m", t=PACK, m=P),
         )
         middle = quantize_weight(round_weight(raw1[1, 0], "scalar"))
         gather_table(1, 0, S)
         first_stage_pass(banks, 1, *middle)
-        last = quantize_weight(round_weight(raw1[2, 0], "scalar"))
+        woven = ring.tile([P, GROUP * PACK], BF16, name="woven", tag="woven", bufs=3, align_bytes=64)
+        for part, half in enumerate(halves):
+            nc.scalar.copy(
+                out=woven[:].rearrange("p (t m i e) -> p m i t e", t=PACK, i=2, e=2)[:, part * P // 2 : (part + 1) * P // 2],
+                in_=half[:].rearrange("p (i e) (m t) -> p m i t e", t=PACK, e=2),
+            )
+        last = quantize_weight(woven)
         for u in range(HALVES):
             gather_table(2, u * BANK, BANK)
         first_stage_pass(banks, 2, *last)
         raw3[0, 0] = load_weight(w3, 0, 0)
         raw3[1, 0] = load_weight(w3, 1, 0, "late", 1)
+        raw3[1, 1] = load_weight(w3, 1, 1)
 
         planes = [[new_planes() for g in range(H_GROUPS)] for i in range(2)]
         w1q = [quantize_weight(round_weight(raw1[0, 1], "vector"))]
 
         def pick_both(g, t):
-            pick(planes[0][g], g, t, pos1_t)
             pick(planes[1][g], g, t, pos2_t)
+            pick(planes[0][g], g, t, pos1_t)
 
         def bias_both(banks, g, t):
             for u in range(HALVES):
@@ -327,61 +341,67 @@ def tile_list_bonsai_vigour_features_kernel(
             bias_both(banks, 1, t)
             pick_both(1, t)
         for i in range(2):
-            quantize_x(i, 0, round_planes(planes[i][0][:], "scalar"))
+            quantize_x(1 - i, 0, round_planes(planes[1 - i][0][:], "scalar"))
             bias_both(banks, 1, 2 + i)
             pick_both(1, 2 + i)
         w3q[1, 0] = quantize_weight(round_weight(raw3[1, 0], "scalar"))
         raw3[0, 1] = load_weight(w3, 0, 1, "late", 1)
-        woven1 = round_planes(planes[0][1][:], "scalar")
-        woven2 = round_planes(planes[1][1][:], "vector")
-        quantize_x(1, 1, woven2)
+        woven2 = round_planes(planes[1][1][:], "scalar")
+        woven1 = round_planes(planes[0][1][:], "vector")
         quantize_x(0, 1, woven1)
+        quantize_x(1, 1, woven2)
         woven = round_weight(raw3[0, 1], "vector")
-        raw3[1, 1] = load_weight(w3, 1, 1, "late", 1)
-        gelu(0, 0, 2)
-        gelu(0, 0, 3)
-        totals = {}
+        for u in range(HALVES):
+            gelu(0, u, 2)
+        waiting = []
         for t in range(PACK):
             take_min(0, t, *second_stage(0, t))
-            totals[t] = finish(0, 0, t)
+            if t == 0:
+                for u in range(HALVES):
+                    gelu(0, u, 3)
+            elif t == 1:
+                w3q[1, 1] = quantize_weight(round_weight(raw3[1, 1], "scalar"))
+            elif t == 2:
+                for row in range(PACK):
+                    gelu(1, 0, row)
+            elif True:
+                for row in range(PACK):
+                    gelu(1, 1, row)
+            for u, row, total in waiting:
+                apply_gain(0, u, row, total)
+            waiting = [(u, t, finish(0, u, t)) for u in range(HALVES)]
             if t == 0:
                 w3q[0, 1] = quantize_weight(woven)
-            else:
-                gelu(*((0, 1, 2), (0, 1, 3), (1, 0, 0))[t - 1])
-                apply_gain(0, 0, t - 1, totals[t - 1])
-        w3q[1, 1] = quantize_weight(round_weight(raw3[1, 1], "scalar"))
-        apply_gain(0, 0, 3, totals[3])
-        store_y(0, 0)
-        for t in range(PACK):
-            totals[t] = finish(0, 1, t)
-            take_min(1, t, *second_stage(1, t))
-            if t == 0:
-                woven_y = round_planes(y[0][0][:], "scalar")
-            else:
-                gelu(1, 0, t)
-                apply_gain(0, 1, t - 1, totals[t - 1])
-        quantize_y(0, 0, woven_y)
-        apply_gain(0, 1, 3, totals[3])
-        store_y(0, 1)
+        take_min(1, 0, *second_stage(1, 0))
+        take_min(1, 1, *second_stage(1, 1))
+        for u, row, total in waiting:
+            apply_gain(0, u, row, total)
+            store_y(0, u)
+        totals = {}
         for t in range(PACK):
             totals[t] = finish(1, 0, t)
-            for u in range(1, len(CHUNKS[1])):
-                gelu(1, u, t)
+            if t < 2:
+                take_min(1, t + 2, *second_stage(1, t + 2))
             if t == 0:
-                woven_y = round_planes(y[0][1][:], "scalar")
+                quantize_y(0, 0, round_planes(y[0][0][:], "scalar"))
             else:
                 apply_gain(1, 0, t - 1, totals[t - 1])
+            if t == 2:
+                woven_y = round_planes(y[0][1][:], "scalar")
+            for u in range(2, len(CHUNKS[1])):
+                gelu(1, u, t)
         quantize_y(0, 1, woven_y)
         store_scales(0)
         apply_gain(1, 0, 3, totals[3])
         store_y(1, 0)
-        woven_y = round_planes(y[1][0][:], "scalar")
-        for u in range(1, len(CHUNKS[1])):
-            last = u == len(CHUNKS[1]) - 1
-            for t in range(PACK):
-                apply_gain(1, u, t, finish(1, u, t), "scalar")
-            store_y(1, u)
-            quantize_y(1, u - 1, woven_y)
-            woven_y = round_planes(y[1][u][:], "vector" if last else "scalar")
-        quantize_y(1, u, woven_y)
+        for t in range(PACK):
+            apply_gain(1, 1, t, finish(1, 1, t))
+        store_y(1, 1)
+        woven_y = [round_planes(y[1][u][:], "scalar") for u in range(2)]
+        for t in range(PACK):
+            apply_gain(1, 2, t, finish(1, 2, t), "vector")
+        store_y(1, 2)
+        woven_y.append(round_planes(y[1][2][:], "vector"))
+        for u in range(3):
+            quantize_y(1, u, woven_y[u])
         store_scales(1)

@@ -20,12 +20,24 @@ P = 128
 PACK = 4
 GROUP = P * PACK
 BANK = 512
-K_PASSES = K // GROUP
+QUADRANT = 32
+QUADRANTS = P // QUADRANT
+SCALE_ROWS = 4
+K_GROUPS = K // GROUP
 H_GROUPS = H // GROUP
 HALVES = S // BANK
 CHUNKS = [[(0, 512), (512, 512)], [(0, 512), (512, 256), (768, 256)]]
 PAD_WINDOW = PADS + 32
 LIST_ROWS = 16
+LINE = 4
+
+RAW_BUFS = 3
+PLANE_BUFS = 3
+WOVEN_BUFS = 3
+WEIGHT_BUFS = 6
+FIRST_BUFS = 2
+TOTAL_BUFS = 4
+Y_CODE_BUFS = 3
 
 
 def tile_list_bonsai_vigour_features_kernel(
@@ -35,21 +47,15 @@ def tile_list_bonsai_vigour_features_kernel(
     with ExitStack() as ctx:
         keep = ctx.enter_context(tc.tile_pool(name="keep", bufs=1))
         ring = ctx.enter_context(tc.tile_pool(name="ring", bufs=1))
-        psum = ctx.enter_context(tc.psum_pool(name="psum", bufs=2))
-
-        def copy_on(engine, out, in_):
-            if engine == "vector":
-                nc.vector.tensor_copy(out=out, in_=in_)
-            else:
-                nc.scalar.copy(out=out, in_=in_)
+        psum = ctx.enter_context(tc.psum_pool(name="psum", bufs=HALVES))
 
         offs_t = keep.tile([P, S // LIST_ROWS], U16, name="offs_t")
         pos1_t = keep.tile([P, PADS // LIST_ROWS], U16, name="pos1_t")
         pos2_t = keep.tile([P, PADS // LIST_ROWS], U16, name="pos2_t")
         pos3_t = keep.tile([P, S // LIST_ROWS], U16, name="pos3_t")
-        tab_w = [keep.tile([P, T], I32, name=f"tab_w{a}", align_bytes=64) for a in range(K_PASSES)]
+        tab_w = [keep.tile([P, T], I32, name=f"tab_w{a}", align_bytes=64) for a in range(K_GROUPS)]
         tab_s = keep.tile([P, T], U8, name="tab_s", align_bytes=64)
-        got_w = [keep.tile([P, S], U32, name=f"got_w{a}", align_bytes=64) for a in range(K_PASSES)]
+        got_w = [keep.tile([P, S], U32, name=f"got_w{a}", align_bytes=64) for a in range(K_GROUPS)]
         got_s = keep.tile([P, S], U8, name="got_s", align_bytes=64)
         w2_raw = keep.tile([P, H_GROUPS, 2 * H], U8, name="w2_raw", align_bytes=64)
         w2_raw_s = keep.tile([P, H_GROUPS, H], U8, name="w2_raw_s", align_bytes=64)
@@ -73,101 +79,120 @@ def tile_list_bonsai_vigour_features_kernel(
             for t in range(PACK):
                 nc.gpsimd.memset(pad[g][t][:, PADS:], 0.0)
 
-        def load_weight(w, a, g, tag="raw", bufs=3):
-            raw = ring.tile([P, PACK, GROUP], F32, name="raw", tag=tag, bufs=bufs, align_bytes=64)
+        def copy_on(engine, out, in_):
+            if engine == "vector":
+                nc.vector.tensor_copy(out=out, in_=in_)
+            else:
+                nc.scalar.copy(out=out, in_=in_)
+
+        def load_rows(tile, w, a, c0, width):
             nc.sync.dma_start(
-                out=raw[:],
-                in_=w[a * GROUP : (a + 1) * GROUP, g * GROUP : (g + 1) * GROUP].rearrange("(p i) c -> p i c", i=PACK),
+                out=tile[:],
+                in_=w[a * GROUP : (a + 1) * GROUP, c0 : c0 + width].rearrange("(p i) c -> p i c", i=PACK),
             )
-            return raw
+            return tile
+
+        def load_weight(w, a, g):
+            raw = ring.tile([P, PACK, GROUP], F32, name="raw", tag="raw", bufs=RAW_BUFS, align_bytes=64)
+            return load_rows(raw, w, a, g * GROUP, GROUP)
+
+        def load_weight_late(w, a, g):
+            raw = ring.tile([P, PACK, GROUP], F32, name="raw", tag="late", bufs=1, align_bytes=64)
+            return load_rows(raw, w, a, g * GROUP, GROUP)
 
         def load_table(a):
             nc.sync.dma_start(out=tab_w[a][:], in_=tab_words[a].rearrange("p c i -> p (c i)").bitcast(I32))
 
+        def load_vector(queue, vec, tile):
+            queue.dma_start(out=tile[:], in_=vec.rearrange("(g p t) -> p g t", p=P, t=PACK))
+
+        def new_woven(columns):
+            return ring.tile([P, columns * PACK], BF16, name="woven", tag="woven", bufs=WOVEN_BUFS, align_bytes=64)
+
+        def dealt(woven):
+            return woven[:].rearrange("p (t m i e) -> p m i t e", t=PACK, i=2, e=2)
+
+        def to_deal(raw):
+            return raw[:].rearrange("p (i e) (m t) -> p m i t e", t=PACK, e=2)
+
         def round_weight(raw, engine):
-            woven = ring.tile([P, GROUP * PACK], BF16, name="woven", tag="woven", bufs=3, align_bytes=64)
-            copy_on(
-                engine,
-                woven[:].rearrange("p (t m i e) -> p m i t e", t=PACK, i=2, e=2),
-                raw[:].rearrange("p (i e) (m t) -> p m i t e", t=PACK, e=2),
-            )
+            woven = new_woven(GROUP)
+            copy_on(engine, dealt(woven), to_deal(raw))
             return woven
 
         def round_planes(planes, engine):
-            woven = ring.tile([P, planes.shape[2] * PACK], BF16, name="woven", tag="woven", bufs=3, align_bytes=64)
+            woven = new_woven(planes.shape[2])
             copy_on(
                 engine,
-                woven[:].rearrange("p (c e t) -> p c t e", t=PACK, e=4),
-                planes.rearrange("p t (c e) -> p c t e", e=4),
+                woven[:].rearrange("p (c e t i) -> p c t e i", t=2, i=2, e=LINE),
+                planes.rearrange("p (t i) (c e) -> p c t e i", i=2, e=LINE),
             )
             return woven
 
         def quantize_weight(woven):
-            codes = ring.tile([P, GROUP], U32, name="w_c", tag="w_c", bufs=6, align_bytes=64)
-            scales = ring.tile([P, GROUP], U8, name="w_s", tag="w_s", bufs=6, align_bytes=64)
+            codes = ring.tile([P, GROUP], U32, name="w_c", tag="w_c", bufs=WEIGHT_BUFS, align_bytes=64)
+            scales = ring.tile([P, GROUP], U8, name="w_s", tag="w_s", bufs=WEIGHT_BUFS, align_bytes=64)
             nc.vector.quantize_mx(out=codes[:].bitcast(E4M3), scales=scales[:], in_=woven[:])
             return codes, scales
 
+        def entries(places, j0, n):
+            return places[:, j0 // LIST_ROWS : (j0 + n) // LIST_ROWS]
+
         def gather_table(a, j0, n):
             nc.vector.tensor_copy(
-                out=got_w[a][:, j0 : j0 + n],
-                in_=tab_w[a][:].bitcast(U32).indirect(offs_t[:, j0 // LIST_ROWS : (j0 + n) // LIST_ROWS]),
+                out=got_w[a][:, j0 : j0 + n], in_=tab_w[a][:].bitcast(U32).indirect(entries(offs_t, j0, n))
             )
-
-        def first_stage_pass(banks, a, codes, scales):
-            for u in range(HALVES):
-                for t in range(PACK):
-                    cols = slice(t * P, (t + 1) * P)
-                    ent = slice(u * BANK, (u + 1) * BANK)
-                    nc.tensor.matmul_mx(
-                        out=banks[t][u][:],
-                        lhsT=codes[:, cols].bitcast(E4M3),
-                        lhsT_scale=scales[:, cols],
-                        rhs=got_w[a][:, ent].bitcast(E4M3),
-                        rhs_scale=got_s[4 * a : P, ent],
-                        start=(a == 0),
-                        stop=(a == K_PASSES - 1),
-                    )
-
-        def first_stage_slice(banks, t, quantized):
-            cols = slice(t * P, (t + 1) * P)
-            for u in range(HALVES):
-                ent = slice(u * BANK, (u + 1) * BANK)
-                for a, (codes, scales) in enumerate(quantized):
-                    nc.tensor.matmul_mx(
-                        out=banks[t][u][:],
-                        lhsT=codes[:, cols].bitcast(E4M3),
-                        lhsT_scale=scales[:, cols],
-                        rhs=got_w[a][:, ent].bitcast(E4M3),
-                        rhs_scale=got_s[4 * a : P, ent],
-                        start=(a == 0),
-                        stop=(a == K_PASSES - 1),
-                    )
 
         def new_banks():
             return [[psum.tile([P, BANK], F32, name="bank", tag=f"bank{t}") for u in range(HALVES)] for t in range(PACK)]
 
+        def first_stage(banks, a, t, u, weight):
+            codes, scales = weight
+            cols = slice(t * P, (t + 1) * P)
+            half = slice(u * BANK, (u + 1) * BANK)
+            nc.tensor.matmul_mx(
+                out=banks[t][u][:],
+                lhsT=codes[:, cols].bitcast(E4M3),
+                lhsT_scale=scales[:, cols],
+                rhs=got_w[a][:, half].bitcast(E4M3),
+                rhs_scale=got_s[SCALE_ROWS * a : P, half],
+                start=(a == 0),
+                stop=(a == K_GROUPS - 1),
+            )
+
+        def first_stage_all_slices(banks, a, weight):
+            for u in range(HALVES):
+                for t in range(PACK):
+                    first_stage(banks, a, t, u, weight)
+
         def add_bias(banks, g, t, u):
             nc.scalar.activation(
-                out=h[g][t][:, u * BANK : (u + 1) * BANK], in_=banks[t][u][:], func=ACT.Identity,
+                out=h[g][t][:, u * BANK : (u + 1) * BANK],
+                in_=banks[t][u][:],
+                func=ACT.Identity,
                 bias=b1_t[:, g, t : t + 1],
             )
+
+        def add_bias_and_pick(banks, g, t):
+            for u in range(HALVES):
+                add_bias(banks, g, t, u)
+            pick(g, t)
+
+        def pick(g, t):
+            for i, places in ((1, pos2_t), (0, pos1_t)):
+                nc.vector.tensor_copy(out=planes[i, g][:, t, :], in_=h[g][t][:].indirect(places[:]))
+
+        def quantize_x(i, g, woven):
+            nc.vector.quantize_mx(out=x_c[i][g][:].bitcast(E4M3), scales=x_s[i][g][:], in_=woven[:])
 
         def gelu(g, u, t):
             j0, n = CHUNKS[g][u]
             nc.scalar.activation(
-                out=y[g][u][:, t, :], in_=h[g][t][:, j0 : j0 + n], func=ACT.Gelu_apprx_tanh,
+                out=y[g][u][:, t, :],
+                in_=h[g][t][:, j0 : j0 + n],
+                func=ACT.Gelu_apprx_tanh,
                 scale=hg_t[:, g, t : t + 1],
             )
-
-        def pick(planes, g, t, places):
-            nc.vector.tensor_copy(out=planes[:, t, :], in_=h[g][t][:].indirect(places[:]))
-
-        def new_planes():
-            return ring.tile([P, PACK, BANK], BF16, name="planes", tag="planes", bufs=4, align_bytes=64)
-
-        def quantize_x(i, g, woven):
-            nc.vector.quantize_mx(out=x_c[i][g][:].bitcast(E4M3), scales=x_s[i][g][:], in_=woven[:])
 
         def second_stage(g, t):
             first = psum.tile([P, BANK], F32, name="bank", tag="bank0")
@@ -194,29 +219,25 @@ def tile_list_bonsai_vigour_features_kernel(
                     start=(a == 0),
                     stop=(a == H_GROUPS - 1),
                 )
-            return first, second
-
-        def take_min(g, t, first, second):
-            first_sb = ring.tile([P, PADS], F32, name="first_sb", tag="first_sb", bufs=2)
+            first_sb = ring.tile([P, PADS], F32, name="first_sb", tag="first_sb", bufs=FIRST_BUFS)
             nc.scalar.copy(out=first_sb[:], in_=first[:])
             nc.vector.tensor_tensor(out=pad[g][t][:, :PADS], in0=second[:], in1=first_sb[:], op=ALU.min)
 
-        def finish(g, u, t, engine="scalar"):
+        def add_pad(g, u, t):
             j0, n = CHUNKS[g][u]
-            total = ring.tile([P, n], F32, name="total", tag="total", bufs=4)
+            total = ring.tile([P, n], F32, name="total", tag="total", bufs=TOTAL_BUFS)
             nc.vector.tensor_tensor(
-                out=total[:], in0=pad[g][t][:].indirect(pos3_t[:, j0 // LIST_ROWS : (j0 + n) // LIST_ROWS]),
-                in1=y[g][u][:, t, :], op=ALU.add,
+                out=total[:], in0=pad[g][t][:].indirect(entries(pos3_t, j0, n)), in1=y[g][u][:, t, :], op=ALU.add
             )
             return total
 
         def apply_gain(g, u, t, total, engine="scalar"):
-            if engine == "scalar":
-                nc.scalar.activation(out=y[g][u][:, t, :], in_=total[:], func=ACT.Copy, scale=gain_t[:, g, t : t + 1])
-            else:
+            if engine == "vector":
                 nc.vector.tensor_scalar(
                     out=y[g][u][:, t, :], in0=total[:], scalar1=gain_t[:, g, t : t + 1], scalar2=None, op0=ALU.mult
                 )
+            else:
+                nc.scalar.activation(out=y[g][u][:, t, :], in_=total[:], func=ACT.Copy, scale=gain_t[:, g, t : t + 1])
 
         def store_y(g, u):
             j0, n = CHUNKS[g][u]
@@ -226,54 +247,47 @@ def tile_list_bonsai_vigour_features_kernel(
 
         def quantize_y(g, u, woven):
             j0, n = CHUNKS[g][u]
-            y_c = ring.tile([P, n], U32, name="y_c", tag="y_c", bufs=3, align_bytes=64)
+            y_c = ring.tile([P, n], U32, name="y_c", tag="y_c", bufs=Y_CODE_BUFS, align_bytes=64)
             nc.vector.quantize_mx(out=y_c[:].bitcast(E4M3), scales=y_s[g][:, j0 : j0 + n], in_=woven[:])
             nc.sync.dma_start(
                 out=out_1[g][:, j0 : j0 + n, :].rearrange("p m t -> p (m t)").bitcast(I32), in_=y_c[:].bitcast(I32)
             )
 
-        def store_scales(g):
-            for q in range(4):
-                (nc.scalar if g == H_GROUPS - 1 and q % 2 else nc.sync).dma_start(
-                    out=out_2[g, 4 * q : 4 * q + 4, :].bitcast(I32), in_=y_s[g][32 * q : 32 * q + 4, :].bitcast(I32)
+        def store_scales(g, queues):
+            for q in range(QUADRANTS):
+                queues[q % len(queues)].dma_start(
+                    out=out_2[g, SCALE_ROWS * q : SCALE_ROWS * (q + 1), :].bitcast(I32),
+                    in_=y_s[g][QUADRANT * q : QUADRANT * q + SCALE_ROWS, :].bitcast(I32),
                 )
 
         raw1 = {}
         raw3 = {}
-
-        def load_vector(queue, vec, tile):
-            queue.dma_start(out=tile[:], in_=vec.rearrange("(g p t) -> p g t", p=P, t=PACK))
-
         nc.sync.dma_start(offs_t[:], offs)
         load_vector(nc.scalar, b1, b1_t)
         load_table(0)
-        for q in range(4):
+        for q in range(QUADRANTS):
             nc.scalar.dma_start(
-                out=tab_s[32 * q : 32 * q + 4 * K_PASSES, :].bitcast(I32),
-                in_=tab_scales[:, 4 * q : 4 * q + 4, :].bitcast(I32),
+                out=tab_s[QUADRANT * q : QUADRANT * q + SCALE_ROWS * K_GROUPS, :].bitcast(I32),
+                in_=tab_scales[:, SCALE_ROWS * q : SCALE_ROWS * (q + 1), :].bitcast(I32),
             )
         nc.scalar.activation(out=warm[:, 4:5], in_=warm[:, 0:1], func=ACT.Gelu_apprx_tanh)
         load_vector(nc.gpsimd, hg, hg_t)
         load_vector(nc.gpsimd, gain, gain_t)
         raw1[0, 0] = load_weight(w1, 0, 0)
         nc.sync.dma_start(out=w2_raw[:].bitcast(I32), in_=w2_words.rearrange("a p c -> p a c").bitcast(I32))
-        for q in range(4):
+        for q in range(QUADRANTS):
             nc.sync.dma_start(
-                out=w2_raw_s[32 * q : 32 * q + 4, :, :].bitcast(I32),
-                in_=w2_scales[:, 4 * q : 4 * q + 4, :].rearrange("a r c -> r a c").bitcast(I32),
+                out=w2_raw_s[QUADRANT * q : QUADRANT * q + SCALE_ROWS, :, :].bitcast(I32),
+                in_=w2_scales[:, SCALE_ROWS * q : SCALE_ROWS * (q + 1), :].rearrange("a r c -> r a c").bitcast(I32),
             )
         raw1[1, 0] = load_weight(w1, 1, 0)
         load_table(1)
-        halves = []
+        parts = []
         for part in range(2):
-            half = ring.tile([P, PACK, GROUP // 2], F32, name="half", tag="planes", bufs=4, align_bytes=64)
-            nc.sync.dma_start(
-                out=half[:],
-                in_=w1[2 * GROUP :, part * GROUP // 2 : (part + 1) * GROUP // 2].rearrange("(p i) c -> p i c", i=PACK),
-            )
-            halves.append(half)
+            tile = ring.tile([P, PACK, GROUP // 2], F32, name="half", tag="planes", bufs=PLANE_BUFS, align_bytes=64)
+            parts.append(load_rows(tile, w1, 2, part * GROUP // 2, GROUP // 2))
         load_table(2)
-        raw1[0, 1] = load_weight(w1, 0, 1, "late", 1)
+        raw1[0, 1] = load_weight_late(w1, 0, 1)
         nc.sync.dma_start(pos1_t[:], pos1)
         nc.sync.dma_start(pos2_t[:], pos2)
         raw1[1, 1] = load_weight(w1, 1, 1)
@@ -284,7 +298,7 @@ def tile_list_bonsai_vigour_features_kernel(
         gather_table(0, 0, S)
         woven = round_weight(raw1[0, 0], "scalar")
         nc.vector.tensor_copy(out=got_s[:], in_=tab_s[:].indirect(offs_t[:]))
-        first_stage_pass(banks, 0, *quantize_weight(woven))
+        first_stage_all_slices(banks, 0, quantize_weight(woven))
         nc.vector.tensor_copy(
             out=w2_c[:].bitcast(U16).rearrange("p a (g t m) -> p (a g) t m", t=PACK, m=P),
             in_=w2_raw[:].bitcast(U16).rearrange("p a (g m t) -> p (a g) t m", t=PACK, m=P),
@@ -293,115 +307,106 @@ def tile_list_bonsai_vigour_features_kernel(
             out=w2_s[:].rearrange("p a (g t m) -> p (a g) t m", t=PACK, m=P),
             in_=w2_raw_s[:].rearrange("p a (g m t) -> p (a g) t m", t=PACK, m=P),
         )
-        middle = quantize_weight(round_weight(raw1[1, 0], "scalar"))
+        weight = quantize_weight(round_weight(raw1[1, 0], "scalar"))
         gather_table(1, 0, S)
-        first_stage_pass(banks, 1, *middle)
-        woven = ring.tile([P, GROUP * PACK], BF16, name="woven", tag="woven", bufs=3, align_bytes=64)
-        for part, half in enumerate(halves):
-            nc.scalar.copy(
-                out=woven[:].rearrange("p (t m i e) -> p m i t e", t=PACK, i=2, e=2)[:, part * P // 2 : (part + 1) * P // 2],
-                in_=half[:].rearrange("p (i e) (m t) -> p m i t e", t=PACK, e=2),
-            )
-        last = quantize_weight(woven)
+        first_stage_all_slices(banks, 1, weight)
+        woven = new_woven(GROUP)
+        for part, tile in enumerate(parts):
+            nc.scalar.copy(out=dealt(woven)[:, part * P // 2 : (part + 1) * P // 2], in_=to_deal(tile))
+        weight = quantize_weight(woven)
         for u in range(HALVES):
             gather_table(2, u * BANK, BANK)
-        first_stage_pass(banks, 2, *last)
+        first_stage_all_slices(banks, 2, weight)
         raw3[0, 0] = load_weight(w3, 0, 0)
-        raw3[1, 0] = load_weight(w3, 1, 0, "late", 1)
+        raw3[1, 0] = load_weight_late(w3, 1, 0)
+        raw3[0, 1] = load_weight(w3, 0, 1)
         raw3[1, 1] = load_weight(w3, 1, 1)
 
-        planes = [[new_planes() for g in range(H_GROUPS)] for i in range(2)]
+        planes = {
+            (i, g): ring.tile([P, PACK, PADS], BF16, name="planes", tag="planes", bufs=PLANE_BUFS, align_bytes=64)
+            for i, g in ((0, 0), (0, 1), (1, 0))
+        }
+        planes[1, 1] = ring.tile([P, PACK, PADS], BF16, name="planes", tag="last_planes", bufs=1, align_bytes=64)
         w1q = [quantize_weight(round_weight(raw1[0, 1], "vector"))]
-
-        def pick_both(g, t):
-            pick(planes[1][g], g, t, pos2_t)
-            pick(planes[0][g], g, t, pos1_t)
-
-        def bias_both(banks, g, t):
-            for u in range(HALVES):
-                add_bias(banks, g, t, u)
-
-        for t, u in ((0, 0), (1, 0), (0, 1), (1, 1)):
-            add_bias(banks, 0, t, u)
-        pick_both(0, 0)
-        pick_both(0, 1)
+        for u in range(HALVES):
+            for t in (0, 1):
+                add_bias(banks, 0, t, u)
+        for t in (0, 1):
+            pick(0, t)
         for t in (0, 1):
             for u in range(HALVES):
                 gelu(0, u, t)
         for a in (1, 2):
             w1q.append(quantize_weight(round_weight(raw1[a, 1], "scalar")))
-            bias_both(banks, 0, a + 1)
-            pick_both(0, a + 1)
+            add_bias_and_pick(banks, 0, a + 1)
+
         banks = new_banks()
         for t in range(PACK):
-            first_stage_slice(banks, t, w1q)
-        w3q = {}
-        w3q[0, 0] = quantize_weight(round_weight(raw3[0, 0], "scalar"))
+            for u in range(HALVES):
+                for a in range(K_GROUPS):
+                    first_stage(banks, a, t, u, w1q[a])
+        w3q = {(0, 0): quantize_weight(round_weight(raw3[0, 0], "scalar"))}
         for t in (0, 1):
-            bias_both(banks, 1, t)
-            pick_both(1, t)
-        for i in range(2):
-            quantize_x(1 - i, 0, round_planes(planes[1 - i][0][:], "scalar"))
-            bias_both(banks, 1, 2 + i)
-            pick_both(1, 2 + i)
+            add_bias_and_pick(banks, 1, t)
+        for i, t in ((1, 2), (0, 3)):
+            quantize_x(i, 0, round_planes(planes[i, 0][:], "scalar"))
+            add_bias_and_pick(banks, 1, t)
         w3q[1, 0] = quantize_weight(round_weight(raw3[1, 0], "scalar"))
-        raw3[0, 1] = load_weight(w3, 0, 1, "late", 1)
-        woven2 = round_planes(planes[1][1][:], "scalar")
-        woven1 = round_planes(planes[0][1][:], "vector")
+        woven2 = round_planes(planes[1, 1][:], "scalar")
+        woven1 = round_planes(planes[0, 1][:], "vector")
         quantize_x(0, 1, woven1)
         quantize_x(1, 1, woven2)
-        woven = round_weight(raw3[0, 1], "vector")
+        woven = ring.tile([P, GROUP * PACK], BF16, name="woven", tag="last_planes", bufs=1, align_bytes=64)
+        nc.vector.tensor_copy(out=dealt(woven), in_=to_deal(raw3[0, 1]))
         for u in range(HALVES):
             gelu(0, u, 2)
+
         waiting = []
         for t in range(PACK):
-            take_min(0, t, *second_stage(0, t))
+            second_stage(0, t)
             if t == 0:
                 for u in range(HALVES):
                     gelu(0, u, 3)
             elif t == 1:
                 w3q[1, 1] = quantize_weight(round_weight(raw3[1, 1], "scalar"))
-            elif t == 2:
+            else:
                 for row in range(PACK):
-                    gelu(1, 0, row)
-            elif True:
-                for row in range(PACK):
-                    gelu(1, 1, row)
+                    gelu(1, t - 2, row)
             for u, row, total in waiting:
                 apply_gain(0, u, row, total)
-            waiting = [(u, t, finish(0, u, t)) for u in range(HALVES)]
+            waiting = [(u, t, add_pad(0, u, t)) for u in range(HALVES)]
             if t == 0:
                 w3q[0, 1] = quantize_weight(woven)
-        take_min(1, 0, *second_stage(1, 0))
-        take_min(1, 1, *second_stage(1, 1))
+
+        second_stage(1, 0)
+        second_stage(1, 1)
         for u, row, total in waiting:
             apply_gain(0, u, row, total)
             store_y(0, u)
-        totals = {}
+        totals = []
         for t in range(PACK):
-            totals[t] = finish(1, 0, t)
-            if t < 2:
-                take_min(1, t + 2, *second_stage(1, t + 2))
+            totals.append(add_pad(1, 0, t))
+            if t + 2 < PACK:
+                second_stage(1, t + 2)
             if t == 0:
                 quantize_y(0, 0, round_planes(y[0][0][:], "scalar"))
             else:
                 apply_gain(1, 0, t - 1, totals[t - 1])
             if t == 2:
-                woven_y = round_planes(y[0][1][:], "scalar")
-            for u in range(2, len(CHUNKS[1])):
-                gelu(1, u, t)
-        quantize_y(0, 1, woven_y)
-        store_scales(0)
-        apply_gain(1, 0, 3, totals[3])
+                woven = round_planes(y[0][1][:], "scalar")
+            gelu(1, 2, t)
+        quantize_y(0, 1, woven)
+        store_scales(0, [nc.sync])
+        apply_gain(1, 0, PACK - 1, totals[PACK - 1])
         store_y(1, 0)
         for t in range(PACK):
-            apply_gain(1, 1, t, finish(1, 1, t))
+            apply_gain(1, 1, t, add_pad(1, 1, t))
         store_y(1, 1)
-        woven_y = [round_planes(y[1][u][:], "scalar") for u in range(2)]
+        rounded = [round_planes(y[1][u][:], "scalar") for u in range(2)]
         for t in range(PACK):
-            apply_gain(1, 2, t, finish(1, 2, t), "vector")
+            apply_gain(1, 2, t, add_pad(1, 2, t), "vector")
         store_y(1, 2)
-        woven_y.append(round_planes(y[1][2][:], "vector"))
-        for u in range(3):
-            quantize_y(1, u, woven_y[u])
-        store_scales(1)
+        rounded.append(round_planes(y[1][2][:], "vector"))
+        for u, woven in enumerate(rounded):
+            quantize_y(1, u, woven)
+        store_scales(1, [nc.sync, nc.scalar])

from contextlib import ExitStack

import concourse.mybir as mybir

K, T, S, PADS, H = 1536, 2048, 1024, 512, 1024
FLOPS = 2 * K * H * S + 2 * 2 * H * H * PADS

F32 = mybir.dt.float32
BF16 = mybir.dt.bfloat16
I32 = mybir.dt.int32
U32 = mybir.dt.uint32
U16 = mybir.dt.uint16
U8 = mybir.dt.uint8
E4M3 = mybir.dt.float8_e4m3fn_x4
E2M1 = mybir.dt.float4_e2m1fn_x4
ACT = mybir.ActivationFunctionType
ALU = mybir.AluOpType

P = 128
PACK = 4
GROUP = P * PACK
BANK = 512
QUADRANT = 32
QUADRANTS = P // QUADRANT
SCALE_ROWS = 4
K_GROUPS = K // GROUP
H_GROUPS = H // GROUP
HALVES = S // BANK
CHUNKS = [[(0, 512), (512, 512)], [(0, 512), (512, 256), (768, 256)]]
PAD_WINDOW = PADS + 32
LIST_ROWS = 16
LINE = 4

RAW_BUFS = 3
PLANE_BUFS = 3
WOVEN_BUFS = 3
WEIGHT_BUFS = 6
FIRST_BUFS = 2
TOTAL_BUFS = 4
Y_CODE_BUFS = 3


def tile_list_bonsai_vigour_features_kernel(
    tc, tab_words, tab_scales, offs, w1, b1, pos1, pos2, w2_words, w2_scales, w3, pos3, hg, gain, out_0, out_1, out_2
):
    nc = tc.nc
    with ExitStack() as ctx:
        keep = ctx.enter_context(tc.tile_pool(name="keep", bufs=1))
        ring = ctx.enter_context(tc.tile_pool(name="ring", bufs=1))
        psum = ctx.enter_context(tc.psum_pool(name="psum", bufs=HALVES))

        offs_t = keep.tile([P, S // LIST_ROWS], U16, name="offs_t")
        pos1_t = keep.tile([P, PADS // LIST_ROWS], U16, name="pos1_t")
        pos2_t = keep.tile([P, PADS // LIST_ROWS], U16, name="pos2_t")
        pos3_t = keep.tile([P, S // LIST_ROWS], U16, name="pos3_t")
        tab_w = [keep.tile([P, T], I32, name=f"tab_w{a}", align_bytes=64) for a in range(K_GROUPS)]
        tab_s = keep.tile([P, T], U8, name="tab_s", align_bytes=64)
        got_w = [keep.tile([P, S], U32, name=f"got_w{a}", align_bytes=64) for a in range(K_GROUPS)]
        got_s = keep.tile([P, S], U8, name="got_s", align_bytes=64)
        w2_raw = keep.tile([P, H_GROUPS, 2 * H], U8, name="w2_raw", align_bytes=64)
        w2_raw_s = keep.tile([P, H_GROUPS, H], U8, name="w2_raw_s", align_bytes=64)
        w2_c = keep.tile([P, H_GROUPS, 2 * H], U8, name="w2_c", align_bytes=64)
        w2_s = keep.tile([P, H_GROUPS, H], U8, name="w2_s", align_bytes=64)
        b1_t = keep.tile([P, H_GROUPS, PACK], F32, name="b1_t")
        hg_t = keep.tile([P, H_GROUPS, PACK], F32, name="hg_t")
        gain_t = keep.tile([P, H_GROUPS, PACK], F32, name="gain_t")
        h = [[keep.tile([P, S], F32, name=f"h{g}{t}") for t in range(PACK)] for g in range(H_GROUPS)]
        y = [[keep.tile([P, PACK, n], F32, name=f"y{g}{j0}") for j0, n in CHUNKS[g]] for g in range(H_GROUPS)]
        pad = [[keep.tile([P, PAD_WINDOW], F32, name=f"pad{g}{t}") for t in range(PACK)] for g in range(H_GROUPS)]
        x_c = [[keep.tile([P, PADS], U32, name=f"x_c{i}{g}", align_bytes=64) for g in range(H_GROUPS)] for i in range(2)]
        x_s = [[keep.tile([P, PADS], U8, name=f"x_s{i}{g}", align_bytes=64) for g in range(H_GROUPS)] for i in range(2)]
        y_s = [keep.tile([P, S], U8, name=f"y_s{g}", align_bytes=64) for g in range(H_GROUPS)]
        warm = keep.tile([P, 8], F32, name="warm")

        nc.vector.memset(tab_s[:].bitcast(I32), 0)
        nc.vector.memset(w2_raw_s[:].rearrange("p a c -> p (a c)").bitcast(I32), 0)
        nc.vector.memset(warm[:], 0.0)
        for g in range(H_GROUPS):
            for t in range(PACK):
                nc.gpsimd.memset(pad[g][t][:, PADS:], 0.0)

        def copy_on(engine, out, in_):
            if engine == "vector":
                nc.vector.tensor_copy(out=out, in_=in_)
            else:
                nc.scalar.copy(out=out, in_=in_)

        def load_rows(tile, w, a, c0, width):
            nc.sync.dma_start(
                out=tile[:],
                in_=w[a * GROUP : (a + 1) * GROUP, c0 : c0 + width].rearrange("(p i) c -> p i c", i=PACK),
            )
            return tile

        def load_weight(w, a, g):
            raw = ring.tile([P, PACK, GROUP], F32, name="raw", tag="raw", bufs=RAW_BUFS, align_bytes=64)
            return load_rows(raw, w, a, g * GROUP, GROUP)

        def load_weight_late(w, a, g):
            raw = ring.tile([P, PACK, GROUP], F32, name="raw", tag="late", bufs=1, align_bytes=64)
            return load_rows(raw, w, a, g * GROUP, GROUP)

        def load_table(a):
            nc.sync.dma_start(out=tab_w[a][:], in_=tab_words[a].rearrange("p c i -> p (c i)").bitcast(I32))

        def load_vector(queue, vec, tile):
            queue.dma_start(out=tile[:], in_=vec.rearrange("(g p t) -> p g t", p=P, t=PACK))

        def new_woven(columns):
            return ring.tile([P, columns * PACK], BF16, name="woven", tag="woven", bufs=WOVEN_BUFS, align_bytes=64)

        def dealt(woven):
            return woven[:].rearrange("p (t m i e) -> p m i t e", t=PACK, i=2, e=2)

        def to_deal(raw):
            return raw[:].rearrange("p (i e) (m t) -> p m i t e", t=PACK, e=2)

        def round_weight(raw, engine):
            woven = new_woven(GROUP)
            copy_on(engine, dealt(woven), to_deal(raw))
            return woven

        def round_planes(planes, engine):
            woven = new_woven(planes.shape[2])
            copy_on(
                engine,
                woven[:].rearrange("p (c e t i) -> p c t e i", t=2, i=2, e=LINE),
                planes.rearrange("p (t i) (c e) -> p c t e i", i=2, e=LINE),
            )
            return woven

        def quantize_weight(woven):
            codes = ring.tile([P, GROUP], U32, name="w_c", tag="w_c", bufs=WEIGHT_BUFS, align_bytes=64)
            scales = ring.tile([P, GROUP], U8, name="w_s", tag="w_s", bufs=WEIGHT_BUFS, align_bytes=64)
            nc.vector.quantize_mx(out=codes[:].bitcast(E4M3), scales=scales[:], in_=woven[:])
            return codes, scales

        def entries(places, j0, n):
            return places[:, j0 // LIST_ROWS : (j0 + n) // LIST_ROWS]

        def gather_table(a, j0, n):
            nc.vector.tensor_copy(
                out=got_w[a][:, j0 : j0 + n], in_=tab_w[a][:].bitcast(U32).indirect(entries(offs_t, j0, n))
            )

        def new_banks():
            return [[psum.tile([P, BANK], F32, name="bank", tag=f"bank{t}") for u in range(HALVES)] for t in range(PACK)]

        def first_stage(banks, a, t, u, weight):
            codes, scales = weight
            cols = slice(t * P, (t + 1) * P)
            half = slice(u * BANK, (u + 1) * BANK)
            nc.tensor.matmul_mx(
                out=banks[t][u][:],
                lhsT=codes[:, cols].bitcast(E4M3),
                lhsT_scale=scales[:, cols],
                rhs=got_w[a][:, half].bitcast(E4M3),
                rhs_scale=got_s[SCALE_ROWS * a : P, half],
                start=(a == 0),
                stop=(a == K_GROUPS - 1),
            )

        def first_stage_all_slices(banks, a, weight):
            for u in range(HALVES):
                for t in range(PACK):
                    first_stage(banks, a, t, u, weight)

        def add_bias(banks, g, t, u):
            nc.scalar.activation(
                out=h[g][t][:, u * BANK : (u + 1) * BANK],
                in_=banks[t][u][:],
                func=ACT.Identity,
                bias=b1_t[:, g, t : t + 1],
            )

        def add_bias_and_pick(banks, g, t):
            for u in range(HALVES):
                add_bias(banks, g, t, u)
            pick(g, t)

        def pick(g, t):
            for i, places in ((1, pos2_t), (0, pos1_t)):
                nc.vector.tensor_copy(out=planes[i, g][:, t, :], in_=h[g][t][:].indirect(places[:]))

        def quantize_x(i, g, woven):
            nc.vector.quantize_mx(out=x_c[i][g][:].bitcast(E4M3), scales=x_s[i][g][:], in_=woven[:])

        def gelu(g, u, t):
            j0, n = CHUNKS[g][u]
            nc.scalar.activation(
                out=y[g][u][:, t, :],
                in_=h[g][t][:, j0 : j0 + n],
                func=ACT.Gelu_apprx_tanh,
                scale=hg_t[:, g, t : t + 1],
            )

        def second_stage(g, t):
            first = psum.tile([P, BANK], F32, name="bank", tag="bank0")
            second = psum.tile([P, BANK], F32, name="bank", tag="bank1")
            c0 = g * GROUP + t * P
            for a in range(H_GROUPS):
                nc.tensor.matmul_mx(
                    out=first[:],
                    lhsT=w2_c[:, a, 2 * c0 : 2 * (c0 + P)].bitcast(E2M1),
                    lhsT_scale=w2_s[:, a, c0 : c0 + P],
                    rhs=x_c[0][a][:].bitcast(E4M3),
                    rhs_scale=x_s[0][a][:],
                    start=(a == 0),
                    stop=(a == H_GROUPS - 1),
                )
            for a in range(H_GROUPS):
                codes, scales = w3q[a, g]
                nc.tensor.matmul_mx(
                    out=second[:],
                    lhsT=codes[:, t * P : (t + 1) * P].bitcast(E4M3),
                    lhsT_scale=scales[:, t * P : (t + 1) * P],
                    rhs=x_c[1][a][:].bitcast(E4M3),
                    rhs_scale=x_s[1][a][:],
                    start=(a == 0),
                    stop=(a == H_GROUPS - 1),
                )
            first_sb = ring.tile([P, PADS], F32, name="first_sb", tag="first_sb", bufs=FIRST_BUFS)
            nc.scalar.copy(out=first_sb[:], in_=first[:])
            nc.vector.tensor_tensor(out=pad[g][t][:, :PADS], in0=second[:], in1=first_sb[:], op=ALU.min)

        def add_pad(g, u, t):
            j0, n = CHUNKS[g][u]
            total = ring.tile([P, n], F32, name="total", tag="total", bufs=TOTAL_BUFS)
            nc.vector.tensor_tensor(
                out=total[:], in0=pad[g][t][:].indirect(entries(pos3_t, j0, n)), in1=y[g][u][:, t, :], op=ALU.add
            )
            return total

        def apply_gain(g, u, t, total, engine="scalar"):
            if engine == "vector":
                nc.vector.tensor_scalar(
                    out=y[g][u][:, t, :], in0=total[:], scalar1=gain_t[:, g, t : t + 1], scalar2=None, op0=ALU.mult
                )
            else:
                nc.scalar.activation(out=y[g][u][:, t, :], in_=total[:], func=ACT.Copy, scale=gain_t[:, g, t : t + 1])

        def store_y(g, u):
            j0, n = CHUNKS[g][u]
            nc.sync.dma_start(
                out=out_0[g * GROUP : (g + 1) * GROUP, j0 : j0 + n].rearrange("(p t) j -> p t j", t=PACK), in_=y[g][u][:]
            )

        def quantize_y(g, u, woven):
            j0, n = CHUNKS[g][u]
            y_c = ring.tile([P, n], U32, name="y_c", tag="y_c", bufs=Y_CODE_BUFS, align_bytes=64)
            nc.vector.quantize_mx(out=y_c[:].bitcast(E4M3), scales=y_s[g][:, j0 : j0 + n], in_=woven[:])
            nc.sync.dma_start(
                out=out_1[g][:, j0 : j0 + n, :].rearrange("p m t -> p (m t)").bitcast(I32), in_=y_c[:].bitcast(I32)
            )

        def store_scales(g, queues):
            for q in range(QUADRANTS):
                queues[q % len(queues)].dma_start(
                    out=out_2[g, SCALE_ROWS * q : SCALE_ROWS * (q + 1), :].bitcast(I32),
                    in_=y_s[g][QUADRANT * q : QUADRANT * q + SCALE_ROWS, :].bitcast(I32),
                )

        raw1 = {}
        raw3 = {}
        nc.sync.dma_start(offs_t[:], offs)
        load_vector(nc.scalar, b1, b1_t)
        load_table(0)
        for q in range(QUADRANTS):
            nc.scalar.dma_start(
                out=tab_s[QUADRANT * q : QUADRANT * q + SCALE_ROWS * K_GROUPS, :].bitcast(I32),
                in_=tab_scales[:, SCALE_ROWS * q : SCALE_ROWS * (q + 1), :].bitcast(I32),
            )
        nc.scalar.activation(out=warm[:, 4:5], in_=warm[:, 0:1], func=ACT.Gelu_apprx_tanh)
        load_vector(nc.gpsimd, hg, hg_t)
        load_vector(nc.gpsimd, gain, gain_t)
        raw1[0, 0] = load_weight(w1, 0, 0)
        nc.sync.dma_start(out=w2_raw[:].bitcast(I32), in_=w2_words.rearrange("a p c -> p a c").bitcast(I32))
        for q in range(QUADRANTS):
            nc.sync.dma_start(
                out=w2_raw_s[QUADRANT * q : QUADRANT * q + SCALE_ROWS, :, :].bitcast(I32),
                in_=w2_scales[:, SCALE_ROWS * q : SCALE_ROWS * (q + 1), :].rearrange("a r c -> r a c").bitcast(I32),
            )
        raw1[1, 0] = load_weight(w1, 1, 0)
        load_table(1)
        parts = []
        for part in range(2):
            tile = ring.tile([P, PACK, GROUP // 2], F32, name="half", tag="planes", bufs=PLANE_BUFS, align_bytes=64)
            parts.append(load_rows(tile, w1, 2, part * GROUP // 2, GROUP // 2))
        load_table(2)
        raw1[0, 1] = load_weight_late(w1, 0, 1)
        nc.sync.dma_start(pos1_t[:], pos1)
        nc.sync.dma_start(pos2_t[:], pos2)
        raw1[1, 1] = load_weight(w1, 1, 1)
        raw1[2, 1] = load_weight(w1, 2, 1)
        nc.sync.dma_start(pos3_t[:], pos3)

        banks = new_banks()
        gather_table(0, 0, S)
        woven = round_weight(raw1[0, 0], "scalar")
        nc.vector.tensor_copy(out=got_s[:], in_=tab_s[:].indirect(offs_t[:]))
        first_stage_all_slices(banks, 0, quantize_weight(woven))
        nc.vector.tensor_copy(
            out=w2_c[:].bitcast(U16).rearrange("p a (g t m) -> p (a g) t m", t=PACK, m=P),
            in_=w2_raw[:].bitcast(U16).rearrange("p a (g m t) -> p (a g) t m", t=PACK, m=P),
        )
        nc.vector.tensor_copy(
            out=w2_s[:].rearrange("p a (g t m) -> p (a g) t m", t=PACK, m=P),
            in_=w2_raw_s[:].rearrange("p a (g m t) -> p (a g) t m", t=PACK, m=P),
        )
        weight = quantize_weight(round_weight(raw1[1, 0], "scalar"))
        gather_table(1, 0, S)
        first_stage_all_slices(banks, 1, weight)
        woven = new_woven(GROUP)
        for part, tile in enumerate(parts):
            nc.scalar.copy(out=dealt(woven)[:, part * P // 2 : (part + 1) * P // 2], in_=to_deal(tile))
        weight = quantize_weight(woven)
        for u in range(HALVES):
            gather_table(2, u * BANK, BANK)
        first_stage_all_slices(banks, 2, weight)
        raw3[0, 0] = load_weight(w3, 0, 0)
        raw3[1, 0] = load_weight_late(w3, 1, 0)
        raw3[0, 1] = load_weight(w3, 0, 1)
        raw3[1, 1] = load_weight(w3, 1, 1)

        planes = {
            (i, g): ring.tile([P, PACK, PADS], BF16, name="planes", tag="planes", bufs=PLANE_BUFS, align_bytes=64)
            for i, g in ((0, 0), (0, 1), (1, 0))
        }
        planes[1, 1] = ring.tile([P, PACK, PADS], BF16, name="planes", tag="last_planes", bufs=1, align_bytes=64)
        w1q = [quantize_weight(round_weight(raw1[0, 1], "vector"))]
        for u in range(HALVES):
            for t in (0, 1):
                add_bias(banks, 0, t, u)
        for t in (0, 1):
            pick(0, t)
        for t in (0, 1):
            for u in range(HALVES):
                gelu(0, u, t)
        for a in (1, 2):
            w1q.append(quantize_weight(round_weight(raw1[a, 1], "scalar")))
            add_bias_and_pick(banks, 0, a + 1)

        banks = new_banks()
        for t in range(PACK):
            for u in range(HALVES):
                for a in range(K_GROUPS):
                    first_stage(banks, a, t, u, w1q[a])
        w3q = {(0, 0): quantize_weight(round_weight(raw3[0, 0], "scalar"))}
        for t in (0, 1):
            add_bias_and_pick(banks, 1, t)
        for i, t in ((1, 2), (0, 3)):
            quantize_x(i, 0, round_planes(planes[i, 0][:], "scalar"))
            add_bias_and_pick(banks, 1, t)
        w3q[1, 0] = quantize_weight(round_weight(raw3[1, 0], "scalar"))
        woven2 = round_planes(planes[1, 1][:], "scalar")
        woven1 = round_planes(planes[0, 1][:], "vector")
        quantize_x(0, 1, woven1)
        quantize_x(1, 1, woven2)
        woven = ring.tile([P, GROUP * PACK], BF16, name="woven", tag="last_planes", bufs=1, align_bytes=64)
        nc.vector.tensor_copy(out=dealt(woven), in_=to_deal(raw3[0, 1]))
        for u in range(HALVES):
            gelu(0, u, 2)

        waiting = []
        for t in range(PACK):
            second_stage(0, t)
            if t == 0:
                for u in range(HALVES):
                    gelu(0, u, 3)
            elif t == 1:
                w3q[1, 1] = quantize_weight(round_weight(raw3[1, 1], "scalar"))
            else:
                for row in range(PACK):
                    gelu(1, t - 2, row)
            for u, row, total in waiting:
                apply_gain(0, u, row, total)
            waiting = [(u, t, add_pad(0, u, t)) for u in range(HALVES)]
            if t == 0:
                w3q[0, 1] = quantize_weight(woven)

        second_stage(1, 0)
        second_stage(1, 1)
        for u, row, total in waiting:
            apply_gain(0, u, row, total)
            store_y(0, u)
        totals = []
        for t in range(PACK):
            totals.append(add_pad(1, 0, t))
            if t + 2 < PACK:
                second_stage(1, t + 2)
            if t == 0:
                quantize_y(0, 0, round_planes(y[0][0][:], "scalar"))
            else:
                apply_gain(1, 0, t - 1, totals[t - 1])
            if t == 2:
                woven = round_planes(y[0][1][:], "scalar")
            gelu(1, 2, t)
        quantize_y(0, 1, woven)
        store_scales(0, [nc.sync])
        apply_gain(1, 0, PACK - 1, totals[PACK - 1])
        store_y(1, 0)
        for t in range(PACK):
            apply_gain(1, 1, t, add_pad(1, 1, t))
        store_y(1, 1)
        rounded = [round_planes(y[1][u][:], "scalar") for u in range(2)]
        for t in range(PACK):
            apply_gain(1, 2, t, add_pad(1, 2, t), "vector")
        store_y(1, 2)
        rounded.append(round_planes(y[1][2][:], "vector"))
        for u, woven in enumerate(rounded):
            quantize_y(1, u, woven)
        store_scales(1, [nc.sync, nc.scalar])
